import numpy as np
CORES = [7,391,135,263,15,399,143,271]
N = 8
TK = 256
D = 128 * N
EPS = 0.01
def setup_inputs(rng):
    return {"x": rng.standard_normal((N, 128, TK), dtype=np.float32) * (0.5 + np.abs(rng.standard_normal((1, 1, TK), dtype=np.float32))), "v": rng.standard_normal((N, 128, TK), dtype=np.float32) * (0.5 + np.abs(rng.standard_normal((1, 1, TK), dtype=np.float32)))}
def setup_inputs_big(rng):
    d = setup_inputs(rng)
    for k in ("x", "v"): d[k] = (d[k].astype(np.float32) * 1024.0).astype(d[k].dtype)
    return d
def setup_inputs_small(rng):
    d = setup_inputs(rng)
    for k in ("x",): d[k] = (d[k].astype(np.float32) * (1 / 1024.0)).astype(d[k].dtype)
    return d
def setup_inputs_apart(rng):
    d = setup_inputs(rng)
    f = (10.0 ** rng.permutation(np.linspace(-1.5, 1.5, N))).astype(np.float32).reshape(N, 1, 1)
    for k in ("x", "v"): d[k] = (d[k].astype(np.float32) * f).astype(d[k].dtype)
    return d
def setup_inputs_mixed(rng):
    d = setup_inputs(rng)
    for k in ("x", "v"):
        f = (10.0 ** rng.uniform(-3, 3, (1, 1, TK))).astype(np.float32); shape = rng.integers(3, size=(1, 1, TK))
        x = d[k].astype(np.float32)
        m = x.mean(axis=(0, 1), keepdims=True); level = m + np.sign(x - m) * np.abs(x - m).mean(axis=(0, 1), keepdims=True) * rng.uniform(0.9, 1.1, x.shape).astype(np.float32)
        other = x * np.where(rng.random(x.shape) < 0.5, 0.1, 1.0).astype(np.float32)
        d[k] = (np.where(shape == 1, level, np.where(shape == 2, other, x)) * f).astype(d[k].dtype)
    return d
def reference(x, v):
    X, V = x.astype(np.float64), v.astype(np.float64)
    n = X / np.sqrt((X ** 2).sum(axis=(0, 1)) / D + EPS)
    Z = n + V
    return {"y": (Z / np.sqrt((Z ** 2).sum(axis=(0, 1)) / D + EPS)).astype(np.float32)}

@@ -1,0 +1,218 @@
+from concourse.bass import DstId, RemoteDMATransfer
+from concourse.mybir import AluOpType, ActivationFunctionType
+
+TK = 256
+H = 128
+W = 6
+EPS = 0.01
+N_ENGINES = 8
+
+SCRATCH = {
+    "xs": ("sbuf", [128, TK], "float32"),
+    "vs": ("sbuf", [128, TK], "float32"),
+    "xx": ("sbuf", [128, TK], "float32"),
+    "xv": ("sbuf", [128, TK], "float32"),
+    "vv": ("sbuf", [128, TK], "float32"),
+    "cst": ("sbuf", [128, 4], "float32"),
+    "ident": ("sbuf", [128, 128], "float32"),
+    "mine": ("sbuf", [128, W], "float32"),
+    "land1": ("sbuf", [128, 3 * W], "float32"),
+    "land2": ("sbuf", [128, W], "float32"),
+    "sm": ("sbuf", [128, 48], "float32"),
+    "xT": ("sbuf", [128, TK], "float32"),
+    "u": ("sbuf", [128, TK], "float32"),
+    "z": ("sbuf", [128, TK], "float32"),
+    "dg": ("sbuf", [128, TK], "float32"),
+    "yo": ("sbuf", [128, TK], "float32"),
+    "ps_stat": ("psum", [128, 512], "float32"),
+    "ps_xT": ("psum", [128, 512], "float32"),
+    "ps_vT": ("psum", [128, 512], "float32"),
+    "ps_y0": ("psum", [128, 512], "float32"),
+    "ps_y1": ("psum", [128, 512], "float32"),
+}
+SEMAPHORES = ["ldx", "ldv", "vq", "aq", "pq", "gq", "arr1", "arr2", "sent", "st0", "st1"]
+
+
+def _some_engines(mask, n):
+    out, b = 0, 1
+    while n and b <= mask:
+        if mask & b:
+            out |= b
+            n -= 1
+        b <<= 1
+    return out
+
+
+def _queue(q, sem):
+    n = [0]
+
+    def run(ins_fn):
+        if n[0]:
+            q.wait_ge(sem, n[0])
+        ins_fn().then_inc(sem, 1)
+        n[0] += 1
+        return n[0]
+    return run, n
+
+
+def rank_program(g, core, T, topo):
+    if T.rank_of(core) is None:
+        return
+    OP, FN = AluOpType, ActivationFunctionType
+    sem = T.sem
+    V, ACT, PE, SY = g.vector, g.scalar, g.tensor, g.sync
+    grp = list(T.cores)
+    D = 128 * len(grp)
+
+    def rack(c):
+        return topo.rack(topo.host(c))
+
+    def near(c):
+        return [d for d in grp if d != c and rack(d) == rack(c)]
+
+    def hops(d):
+        return 2 if topo.mates(core, d) else (1 if topo.same_plane(core, d) else 0)
+
+    peers = sorted(near(core), key=hops)
+    far = [d for d in grp if rack(d) != rack(core) and topo.chip(d) == topo.chip(core) and topo.may_write(core, d)][0]
+
+    def dst(d):
+        rid, pid = topo.addr(d, core)
+        return DstId(rid=rid, pnc=pid)
+
+    m1 = topo.mask(core, far)
+    for d in peers:
+        m1 &= topo.mask(core, d)
+    mask = _some_engines(m1, N_ENGINES)
+    ne = bin(mask).count("1")
+
+    v_, nv = _queue(V, sem.vq)
+    a_, na = _queue(ACT, sem.aq)
+    p_, npe = _queue(PE, sem.pq)
+
+    def half(t, h):
+        return t[:, h * H:(h + 1) * H]
+
+    SY.dma_start(T.xs[:], T.x[:]).then_inc(sem.ldx, 16)
+    ACT.dma_start(T.vs[:], T.v[:]).then_inc(sem.ldv, 16)
+
+    v_(lambda: V.memset(T.cst[:, 0:1], 1.0))
+    v_cst = v_(lambda: V.memset(T.cst[:, 1:2], 2.0))
+    v_one = v_(lambda: V.memset(T.ident[:], 1.0))
+    g.wait_ge(sem.vq, v_one)
+    g.affine_select(T.ident[:], T.ident[:], [[-1, 128]], OP.is_equal, 0.0, 0, 1).then_inc(sem.gq, 1)
+
+    ACT.wait_ge(sem.ldx, 16)
+    a_xx = [a_(lambda h=h: ACT.activation(half(T.xx, h), half(T.xs, h), FN.Square)) for h in (0, 1)]
+    ACT.wait_ge(sem.ldv, 16)
+    a_vv = [a_(lambda h=h: ACT.activation(half(T.vv, h), half(T.vs, h), FN.Square)) for h in (0, 1)]
+    V.wait_ge(sem.ldx, 16)
+    V.wait_ge(sem.ldv, 16)
+    v_xv = [v_(lambda h=h: V.tensor_tensor(half(T.xv, h), half(T.xs, h), half(T.vs, h), OP.mult)) for h in (0, 1)]
+
+    def stat(col, prod, h, c):
+        return p_(lambda: PE.matmul(T.ps_stat[:, col:col + 1], half(prod, h), T.cst[:, c:c + 1], True, True))
+
+    PE.wait_ge(sem.vq, v_cst)
+    for h in (0, 1):
+        PE.wait_ge(sem.aq, a_xx[h])
+        stat(0 + h, T.xx, h, 0)
+    for h in (0, 1):
+        PE.wait_ge(sem.aq, a_vv[h])
+        stat(4 + h, T.vv, h, 0)
+        PE.wait_ge(sem.vq, v_xv[h])
+        p_stat = stat(2 + h, T.xv, h, 1)
+    V.wait_ge(sem.pq, p_stat)
+    v_mine = v_(lambda: V.tensor_copy(T.mine[:], T.ps_stat[:, 0:W]))
+
+    g.wait_ge(sem.vq, v_mine)
+    g.remote_dma_fused([RemoteDMATransfer(
+        dst_ids=[dst(d) for d in peers], dma_engine_mask=mask, remote_sem=sem.arr1, srcs=[T.mine[:]],
+        dsts=[T.land1[:, W * near(d).index(core):W * near(d).index(core) + W] for d in peers], alu_op=0)],
+        local_sem=sem.sent)
+
+    PE.wait_ge(sem.gq, 1)
+    for h in (0, 1):
+        p_xT = p_(lambda h=h: PE.matmul(half(T.ps_xT, h), half(T.xs, h), T.ident[:], True, True))
+    for h in (0, 1):
+        p_vT = p_(lambda h=h: PE.matmul(half(T.ps_vT, h), half(T.vs, h), T.ident[:], True, True))
+    ACT.wait_ge(sem.pq, p_xT)
+    a_(lambda: ACT.activation(T.xT[:], T.ps_xT[:, 0:TK], FN.Copy))
+
+    g.wait_ge(sem.arr1, 3 * ne)
+    g.remote_dma_fused([RemoteDMATransfer(
+        dst_ids=[dst(far)], dma_engine_mask=mask, remote_sem=sem.arr2,
+        srcs=[T.mine[:]] + [T.land1[:, W * k:W * k + W] for k in range(3)], dsts=[T.land2[:]], alu_op=1)],
+        local_sem=sem.sent)
+
+    sm = T.sm
+    R, S, t6 = sm[:, 0:6], sm[:, 8:14], sm[:, 40:46]
+    SA, SB, SC = sm[:, 8:10], sm[:, 10:12], sm[:, 12:14]
+    w, m, r, t, s = sm[:, 16:18], sm[:, 18:20], sm[:, 20:22], sm[:, 22:24], sm[:, 24:26]
+    q, w2, m2, r2, s2 = sm[:, 26:28], sm[:, 28:30], sm[:, 30:32], sm[:, 32:34], sm[:, 36:38]
+
+    def tt(o, a, b, op):
+        return v_(lambda: V.tensor_tensor(o, a, b, op))
+
+    V.wait_ge(sem.arr1, 3 * ne)
+    tt(t6, T.land1[:, 0:W], T.land1[:, W:2 * W], OP.add)
+    tt(R, T.land1[:, 2 * W:3 * W], T.mine[:], OP.add)
+    tt(R, R, t6, OP.add)
+
+    def rsqrt(src, w_, m_, r_, out, fill=None):
+        ACT.wait_ge(sem.vq, nv[0])
+        a_w = a_(lambda: ACT.activation(w_, src, FN.Sqrt, bias=EPS, scale=1.0 / D))
+        v_(lambda: V.tensor_scalar(m_, src, 1.0 / D, EPS, OP.mult, OP.add))
+        if fill:
+            fill()
+        V.wait_ge(sem.aq, a_w)
+        v_(lambda: V.reciprocal(r_, w_))
+        tt(t, r_, m_, OP.mult)
+        tt(t, t, r_, OP.mult)
+        v_(lambda: V.tensor_scalar(t, t, -0.5, 1.5, OP.mult, OP.add))
+        return tt(out, r_, t, OP.mult)
+
+    V.wait_ge(sem.arr2, ne)
+    tt(S, R, T.land2[:], OP.add)
+    v_s = rsqrt(SA, w, m, r, s)
+
+    ACT.wait_ge(sem.vq, v_s)
+    a_u = [a_(lambda h=h: ACT.activation(half(T.u, h), half(T.xT, h), FN.Identity, scale=sm[:, 24 + h:25 + h]))
+           for h in (0, 1)]
+    tt(t, s, SA, OP.mult)
+    tt(t, t, SB, OP.add)
+    tt(t, t, s, OP.mult)
+    tt(q, t, SC, OP.add)
+
+    def zT(h):
+        V.wait_ge(sem.aq, a_u[h])
+        V.wait_ge(sem.pq, p_vT)
+        return tt(half(T.z, h), half(T.u, h), half(T.ps_vT, h), OP.add)
+
+    v_s2 = rsqrt(q, w2, m2, r2, s2, fill=lambda: zT(0))
+
+    ACT.wait_ge(sem.vq, v_s2)
+    a_dg1 = a_(lambda: ACT.activation(half(T.dg, 1), T.ident[:], FN.Identity, scale=sm[:, 37:38]))
+    v_dg0 = v_(lambda: V.tensor_scalar(half(T.dg, 0), T.ident[:], sm[:, 36:37], None, OP.mult))
+    v_z1 = zT(1)
+    PE.wait_ge(sem.vq, v_dg0)
+    p_y0 = p_(lambda: PE.matmul(T.ps_y0[:, 0:H], half(T.z, 0), half(T.dg, 0), True, True))
+    PE.wait_ge(sem.vq, v_z1)
+    PE.wait_ge(sem.aq, a_dg1)
+    p_y1 = p_(lambda: PE.matmul(T.ps_y1[:, 0:H], half(T.z, 1), half(T.dg, 1), True, True))
+
+    V.wait_ge(sem.pq, p_y0)
+    v_y0 = v_(lambda: V.tensor_copy(half(T.yo, 0), T.ps_y0[:, 0:H]))
+    SY.wait_ge(sem.vq, v_y0)
+    SY.dma_start(half(T.y, 0), half(T.yo, 0)).then_inc(sem.st0, 16)
+    ACT.wait_ge(sem.pq, p_y1)
+    a_y1 = a_(lambda: ACT.activation(half(T.yo, 1), T.ps_y1[:, 0:H], FN.Copy))
+    ACT.wait_ge(sem.aq, a_y1)
+    ACT.dma_start(half(T.y, 1), half(T.yo, 1)).then_inc(sem.st1, 16)
+
+    g.wait_ge(sem.sent, 2 * ne)
+    g.wait_ge(sem.vq, nv[0])
+    g.wait_ge(sem.aq, na[0])
+    g.wait_ge(sem.pq, npe[0])
+    g.wait_ge(sem.st0, 16)
+    g.wait_ge(sem.st1, 16)

@@ -3,9 +3,11 @@ from concourse.mybir import AluOpType, ActivationFunctionType
 
 TK = 256
 H = 128
-W = 6
+W = 8
 EPS = 0.01
+DOWN = 2.0 ** -4
 N_ENGINES = 8
+N_STAGES = 48
 
 SCRATCH = {
     "xs": ("sbuf", [128, TK], "float32"),
@@ -14,23 +16,26 @@ SCRATCH = {
     "xv": ("sbuf", [128, TK], "float32"),
     "vv": ("sbuf", [128, TK], "float32"),
     "cst": ("sbuf", [128, 4], "float32"),
+    "epsv": ("sbuf", [128, W], "float32"),
     "ident": ("sbuf", [128, 128], "float32"),
+    "identn": ("sbuf", [128, 128], "float32"),
     "mine": ("sbuf", [128, W], "float32"),
     "land1": ("sbuf", [128, 3 * W], "float32"),
     "land2": ("sbuf", [128, W], "float32"),
-    "sm": ("sbuf", [128, 48], "float32"),
+    "sm": ("sbuf", [128, 96], "float32"),
     "xT": ("sbuf", [128, TK], "float32"),
     "u": ("sbuf", [128, TK], "float32"),
     "z": ("sbuf", [128, TK], "float32"),
     "dg": ("sbuf", [128, TK], "float32"),
     "yo": ("sbuf", [128, TK], "float32"),
-    "ps_stat": ("psum", [128, 512], "float32"),
+    "ps_a": ("psum", [128, 512], "float32"),
+    "ps_bc": ("psum", [128, 512], "float32"),
     "ps_xT": ("psum", [128, 512], "float32"),
     "ps_vT": ("psum", [128, 512], "float32"),
     "ps_y0": ("psum", [128, 512], "float32"),
     "ps_y1": ("psum", [128, 512], "float32"),
 }
-SEMAPHORES = ["ldx", "ldv", "vq", "aq", "pq", "gq", "arr1", "arr2", "sent", "st0", "st1"]
+SEMAPHORES = ["ldx", "ldv", "arr1", "arr2", "sent", "st0", "st1"] + ["s%d" % i for i in range(N_STAGES)]
 
 
 def _some_engines(mask, n):
@@ -41,18 +46,6 @@ def _some_engines(mask, n):
             n -= 1
         b <<= 1
     return out
-
-
-def _queue(q, sem):
-    n = [0]
-
-    def run(ins_fn):
-        if n[0]:
-            q.wait_ge(sem, n[0])
-        ins_fn().then_inc(sem, 1)
-        n[0] += 1
-        return n[0]
-    return run, n
 
 
 def rank_program(g, core, T, topo):
@@ -86,133 +79,143 @@ def rank_program(g, core, T, topo):
     mask = _some_engines(m1, N_ENGINES)
     ne = bin(mask).count("1")
 
-    v_, nv = _queue(V, sem.vq)
-    a_, na = _queue(ACT, sem.aq)
-    p_, npe = _queue(PE, sem.pq)
+    stages = []
 
-    def half(t, h):
-        return t[:, h * H:(h + 1) * H]
+    def stage():
+        st = [sem["s%d" % len(stages)], 0]
+        stages.append(st)
+        return st
+
+    def do(q, deps, st, fn):
+        for d in deps:
+            q.wait_ge(d[0], d[1])
+        fn().then_inc(st[0], 1)
+        st[1] += 1
+
+    def one(q, deps, fn):
+        st = stage()
+        do(q, deps, st, fn)
+        return st
+
+    def two(q, deps, fn):
+        st = stage()
+        do(q, deps, st, lambda: fn(0))
+        do(q, [], st, lambda: fn(1))
+        return st
+
+    def half(t_, h):
+        return t_[:, h * H:(h + 1) * H]
+
+    sm = T.sm
+
+    def col(base, h=None):
+        return sm[:, base:base + 2] if h is None else sm[:, base + h:base + h + 1]
+
+    def ts(o, i, s1, s2, o1, o2):
+        return V.tensor_scalar(o, i, s1, s2, o1, o2)
+
+    LDX, LDV = [sem.ldx, 16], [sem.ldv, 16]
+    ARR1, ARR2 = [sem.arr1, 3 * ne], [sem.arr2, ne]
 
     SY.dma_start(T.xs[:], T.x[:]).then_inc(sem.ldx, 16)
     ACT.dma_start(T.vs[:], T.v[:]).then_inc(sem.ldv, 16)
 
-    v_(lambda: V.memset(T.cst[:, 0:1], 1.0))
-    v_cst = v_(lambda: V.memset(T.cst[:, 1:2], 2.0))
-    v_one = v_(lambda: V.memset(T.ident[:], 1.0))
-    g.wait_ge(sem.vq, v_one)
-    g.affine_select(T.ident[:], T.ident[:], [[-1, 128]], OP.is_equal, 0.0, 0, 1).then_inc(sem.gq, 1)
+    K = stage()
+    for ap, val in ((T.cst[:, 0:1], 1.0 / D), (T.cst[:, 1:2], 0.25 / D), (T.cst[:, 2:3], -1.0 / D),
+                    (T.ident[:], 1.0), (T.identn[:], -0.5),
+                    (T.epsv[:, 0:1], EPS), (T.epsv[:, 1:2], 0.0), (T.epsv[:, 2:3], EPS), (T.epsv[:, 3:6], 0.0),
+                    (T.epsv[:, 6:8], EPS)):
+        do(V, [], K, lambda ap=ap, val=val: V.memset(ap, val))
+    G = stage()
+    do(g, [K], G, lambda: g.affine_select(T.identn[:], T.identn[:], [[-1, 128]], OP.is_equal, 0.0, 0, 1))
+    do(g, [], G, lambda: g.affine_select(T.ident[:], T.ident[:], [[-1, 128]], OP.is_equal, 0.0, 0, 1))
 
-    ACT.wait_ge(sem.ldx, 16)
-    a_xx = [a_(lambda h=h: ACT.activation(half(T.xx, h), half(T.xs, h), FN.Square)) for h in (0, 1)]
-    ACT.wait_ge(sem.ldv, 16)
-    a_vv = [a_(lambda h=h: ACT.activation(half(T.vv, h), half(T.vs, h), FN.Square)) for h in (0, 1)]
-    V.wait_ge(sem.ldx, 16)
-    V.wait_ge(sem.ldv, 16)
-    v_xv = [v_(lambda h=h: V.tensor_tensor(half(T.xv, h), half(T.xs, h), half(T.vs, h), OP.mult)) for h in (0, 1)]
+    XX = [one(ACT, [LDX], lambda h=h: ACT.activation(half(T.xx, h), half(T.xs, h), FN.Square)) for h in (0, 1)]
+    VV = [one(ACT, [LDV], lambda h=h: ACT.activation(half(T.vv, h), half(T.vs, h), FN.Square)) for h in (0, 1)]
+    XV = one(V, [LDX, LDV], lambda: V.tensor_tensor(T.xv[:], T.xs[:], T.vs[:], OP.mult))
 
-    def stat(col, prod, h, c):
-        return p_(lambda: PE.matmul(T.ps_stat[:, col:col + 1], half(prod, h), T.cst[:, c:c + 1], True, True))
-
-    PE.wait_ge(sem.vq, v_cst)
+    PA, PBC = stage(), stage()
     for h in (0, 1):
-        PE.wait_ge(sem.aq, a_xx[h])
-        stat(0 + h, T.xx, h, 0)
+        do(PE, [K, XX[h]], PA, lambda h=h: PE.matmul(T.ps_a[:, 2 * h:2 * h + 2], half(T.xx, h), T.cst[:, 0:2], True, True))
     for h in (0, 1):
-        PE.wait_ge(sem.aq, a_vv[h])
-        stat(4 + h, T.vv, h, 0)
-        PE.wait_ge(sem.vq, v_xv[h])
-        p_stat = stat(2 + h, T.xv, h, 1)
-    V.wait_ge(sem.pq, p_stat)
-    v_mine = v_(lambda: V.tensor_copy(T.mine[:], T.ps_stat[:, 0:W]))
+        do(PE, [VV[h]], PBC, lambda h=h: PE.matmul(T.ps_bc[:, 2 + h:3 + h], half(T.vv, h), T.cst[:, 0:1], True, True))
+    for h in (0, 1):
+        do(PE, [XV], PBC, lambda h=h: PE.matmul(T.ps_bc[:, h:h + 1], half(T.xv, h), T.cst[:, 2:3], True, True))
+    MA = one(ACT, [PA], lambda: ACT.activation(T.mine[:, 0:4], T.ps_a[:, 0:4], FN.Copy))
+    MBC = one(V, [PBC], lambda: V.tensor_copy(T.mine[:, 4:8], T.ps_bc[:, 0:4]))
 
-    g.wait_ge(sem.vq, v_mine)
+    g.wait_ge(MA[0], MA[1])
+    g.wait_ge(MBC[0], MBC[1])
     g.remote_dma_fused([RemoteDMATransfer(
         dst_ids=[dst(d) for d in peers], dma_engine_mask=mask, remote_sem=sem.arr1, srcs=[T.mine[:]],
         dsts=[T.land1[:, W * near(d).index(core):W * near(d).index(core) + W] for d in peers], alu_op=0)],
         local_sem=sem.sent)
 
-    PE.wait_ge(sem.gq, 1)
+    wo, ro = sm[:, 0:4], sm[:, 4:8]
+    WO = one(ACT, [MA], lambda: ACT.activation(wo, T.mine[:, 0:4], FN.Sqrt, bias=EPS, scale=1.0))
+    ME = one(V, [MA, MBC, K], lambda: V.tensor_tensor(sm[:, 8:16], T.mine[:], T.epsv[:], OP.add))
+    RO = one(V, [WO], lambda: V.reciprocal(ro, wo))
+    SC = stage()
     for h in (0, 1):
-        p_xT = p_(lambda h=h: PE.matmul(half(T.ps_xT, h), half(T.xs, h), T.ident[:], True, True))
-    for h in (0, 1):
-        p_vT = p_(lambda h=h: PE.matmul(half(T.ps_vT, h), half(T.vs, h), T.ident[:], True, True))
-    ACT.wait_ge(sem.pq, p_xT)
-    a_(lambda: ACT.activation(T.xT[:], T.ps_xT[:, 0:TK], FN.Copy))
+        do(V, [RO], SC, lambda h=h: ts(col(16, h), sm[:, 4 + 2 * h:5 + 2 * h], sm[:, 4 + 2 * h:5 + 2 * h], DOWN * DOWN,
+                                       OP.mult, OP.mult))
+        do(V, [], SC, lambda h=h: V.tensor_scalar(col(18, h), sm[:, 4 + 2 * h:5 + 2 * h], DOWN, None, OP.mult))
 
-    g.wait_ge(sem.arr1, 3 * ne)
+    PX = two(PE, [G], lambda h: PE.matmul(half(T.ps_xT, h), half(T.xs, h), T.identn[:], True, True))
+    PV = two(PE, [], lambda h: PE.matmul(half(T.ps_vT, h), half(T.vs, h), T.ident[:], True, True))
+    XT = one(ACT, [PX], lambda: ACT.activation(T.xT[:], T.ps_xT[:, 0:TK], FN.Copy))
+
+    g.wait_ge(ARR1[0], ARR1[1])
     g.remote_dma_fused([RemoteDMATransfer(
         dst_ids=[dst(far)], dma_engine_mask=mask, remote_sem=sem.arr2,
         srcs=[T.mine[:]] + [T.land1[:, W * k:W * k + W] for k in range(3)], dsts=[T.land2[:]], alu_op=1)],
         local_sem=sem.sent)
 
-    sm = T.sm
-    R, S, t6 = sm[:, 0:6], sm[:, 8:14], sm[:, 40:46]
-    SA, SB, SC = sm[:, 8:10], sm[:, 10:12], sm[:, 12:14]
-    w, m, r, t, s = sm[:, 16:18], sm[:, 18:20], sm[:, 20:22], sm[:, 22:24], sm[:, 24:26]
-    q, w2, m2, r2, s2 = sm[:, 26:28], sm[:, 28:30], sm[:, 30:32], sm[:, 32:34], sm[:, 36:38]
+    a8, b8, R, S = sm[:, 24:32], sm[:, 32:40], sm[:, 40:48], sm[:, 48:56]
+    AB = stage()
+    do(V, [ARR1], AB, lambda: V.tensor_tensor(a8, T.land1[:, 0:W], T.land1[:, W:2 * W], OP.add))
+    do(V, [ME], AB, lambda: V.tensor_tensor(b8, T.land1[:, 2 * W:3 * W], sm[:, 8:16], OP.add))
+    BS = two(V, [AB, SC], lambda h: ts(col(20, h), sm[:, 24 + 2 * h:25 + 2 * h], sm[:, 32 + 2 * h:33 + 2 * h], col(16, h),
+                                       OP.add, OP.mult))
+    RR = one(V, [], lambda: V.tensor_tensor(R, a8, b8, OP.add))
 
-    def tt(o, a, b, op):
-        return v_(lambda: V.tensor_tensor(o, a, b, op))
+    def landed_a(h):
+        return T.land2[:, 2 * h:2 * h + 1]
 
-    V.wait_ge(sem.arr1, 3 * ne)
-    tt(t6, T.land1[:, 0:W], T.land1[:, W:2 * W], OP.add)
-    tt(R, T.land1[:, 2 * W:3 * W], T.mine[:], OP.add)
-    tt(R, R, t6, OP.add)
+    WW = two(ACT, [BS, ARR2], lambda h: ACT.activation(col(56, h), landed_a(h), FN.Sqrt, bias=col(20, h), scale=col(16, h)))
+    MH = two(V, [ARR2, BS], lambda h: ts(col(58, h), landed_a(h), col(16, h), col(20, h), OP.mult, OP.add))
+    SS = one(V, [RR], lambda: V.tensor_tensor(S, R, T.land2[:], OP.add))
+    RC = one(V, [WW], lambda: V.reciprocal(col(60), col(56)))
+    EE = two(V, [RC, MH], lambda h: ts(col(62, h), col(60, h), col(58, h), col(60, h), OP.mult, OP.mult))
+    do(V, [], EE, lambda: V.tensor_tensor(col(64), col(60), col(18), OP.mult))
+    SP = two(V, [EE], lambda h: ts(col(66, h), col(62, h), 3.0, col(64, h), OP.subtract, OP.mult))
 
-    def rsqrt(src, w_, m_, r_, out, fill=None):
-        ACT.wait_ge(sem.vq, nv[0])
-        a_w = a_(lambda: ACT.activation(w_, src, FN.Sqrt, bias=EPS, scale=1.0 / D))
-        v_(lambda: V.tensor_scalar(m_, src, 1.0 / D, EPS, OP.mult, OP.add))
-        if fill:
-            fill()
-        V.wait_ge(sem.aq, a_w)
-        v_(lambda: V.reciprocal(r_, w_))
-        tt(t, r_, m_, OP.mult)
-        tt(t, t, r_, OP.mult)
-        v_(lambda: V.tensor_scalar(t, t, -0.5, 1.5, OP.mult, OP.add))
-        return tt(out, r_, t, OP.mult)
+    TQ = two(ACT, [SP, SS], lambda h: ACT.activation(col(68, h), sm[:, 49 + 2 * h:50 + 2 * h], FN.Identity,
+                                                     bias=sm[:, 52 + h:53 + h], scale=col(66, h)))
+    W2 = two(ACT, [TQ], lambda h: ACT.activation(col(70, h), col(68, h), FN.Sqrt, bias=sm[:, 54 + h:55 + h],
+                                                 scale=col(66, h)))
+    U0 = one(V, [SP, XT], lambda: V.tensor_scalar(half(T.u, 0), half(T.xT, 0), col(66, 0), None, OP.mult))
+    U1 = one(ACT, [XT], lambda: ACT.activation(half(T.u, 1), half(T.xT, 1), FN.Identity, scale=col(66, 1)))
+    Z0 = one(V, [U0, PV], lambda: V.tensor_tensor(half(T.z, 0), half(T.u, 0), half(T.ps_vT, 0), OP.add))
+    M2 = two(V, [TQ, SS], lambda h: ts(col(72, h), col(68, h), col(66, h), sm[:, 54 + h:55 + h], OP.mult, OP.add))
+    R2 = one(V, [W2], lambda: V.reciprocal(col(74), col(70)))
+    E2 = two(V, [R2, M2], lambda h: ts(col(76, h), col(74, h), col(72, h), col(74, h), OP.mult, OP.mult))
+    S2 = [one(V, [E2], lambda h=h: ts(col(78, h), col(76, h), 3.0, col(74, h), OP.subtract, OP.mult)) for h in (0, 1)]
 
-    V.wait_ge(sem.arr2, ne)
-    tt(S, R, T.land2[:], OP.add)
-    v_s = rsqrt(SA, w, m, r, s)
-
-    ACT.wait_ge(sem.vq, v_s)
-    a_u = [a_(lambda h=h: ACT.activation(half(T.u, h), half(T.xT, h), FN.Identity, scale=sm[:, 24 + h:25 + h]))
-           for h in (0, 1)]
-    tt(t, s, SA, OP.mult)
-    tt(t, t, SB, OP.add)
-    tt(t, t, s, OP.mult)
-    tt(q, t, SC, OP.add)
-
-    def zT(h):
-        V.wait_ge(sem.aq, a_u[h])
-        V.wait_ge(sem.pq, p_vT)
-        return tt(half(T.z, h), half(T.u, h), half(T.ps_vT, h), OP.add)
-
-    v_s2 = rsqrt(q, w2, m2, r2, s2, fill=lambda: zT(0))
-
-    ACT.wait_ge(sem.vq, v_s2)
-    a_dg1 = a_(lambda: ACT.activation(half(T.dg, 1), T.ident[:], FN.Identity, scale=sm[:, 37:38]))
-    v_dg0 = v_(lambda: V.tensor_scalar(half(T.dg, 0), T.ident[:], sm[:, 36:37], None, OP.mult))
-    v_z1 = zT(1)
-    PE.wait_ge(sem.vq, v_dg0)
-    p_y0 = p_(lambda: PE.matmul(T.ps_y0[:, 0:H], half(T.z, 0), half(T.dg, 0), True, True))
-    PE.wait_ge(sem.vq, v_z1)
-    PE.wait_ge(sem.aq, a_dg1)
-    p_y1 = p_(lambda: PE.matmul(T.ps_y1[:, 0:H], half(T.z, 1), half(T.dg, 1), True, True))
-
-    V.wait_ge(sem.pq, p_y0)
-    v_y0 = v_(lambda: V.tensor_copy(half(T.yo, 0), T.ps_y0[:, 0:H]))
-    SY.wait_ge(sem.vq, v_y0)
+    DG0 = one(V, [S2[0], G], lambda: V.tensor_scalar(half(T.dg, 0), T.identn[:], col(78, 0), None, OP.mult))
+    DG1 = one(ACT, [S2[1], G], lambda: ACT.activation(half(T.dg, 1), T.identn[:], FN.Identity, scale=col(78, 1)))
+    Z1 = one(V, [U1], lambda: V.tensor_tensor(half(T.z, 1), half(T.u, 1), half(T.ps_vT, 1), OP.add))
+    Y0 = one(PE, [DG0, Z0], lambda: PE.matmul(T.ps_y0[:, 0:H], half(T.z, 0), half(T.dg, 0), True, True))
+    Y1 = one(PE, [DG1, Z1], lambda: PE.matmul(T.ps_y1[:, 0:H], half(T.z, 1), half(T.dg, 1), True, True))
+    C0 = one(V, [Y0], lambda: V.tensor_copy(half(T.yo, 0), T.ps_y0[:, 0:H]))
+    SY.wait_ge(C0[0], C0[1])
     SY.dma_start(half(T.y, 0), half(T.yo, 0)).then_inc(sem.st0, 16)
-    ACT.wait_ge(sem.pq, p_y1)
-    a_y1 = a_(lambda: ACT.activation(half(T.yo, 1), T.ps_y1[:, 0:H], FN.Copy))
-    ACT.wait_ge(sem.aq, a_y1)
+    C1 = one(ACT, [Y1], lambda: ACT.activation(half(T.yo, 1), T.ps_y1[:, 0:H], FN.Copy))
+    ACT.wait_ge(C1[0], C1[1])
     ACT.dma_start(half(T.y, 1), half(T.yo, 1)).then_inc(sem.st1, 16)
 
     g.wait_ge(sem.sent, 2 * ne)
-    g.wait_ge(sem.vq, nv[0])
-    g.wait_ge(sem.aq, na[0])
-    g.wait_ge(sem.pq, npe[0])
+    for st in stages:
+        g.wait_ge(st[0], st[1])
     g.wait_ge(sem.st0, 16)
     g.wait_ge(sem.st1, 16)

@@ -3,7 +3,7 @@ from concourse.mybir import AluOpType, ActivationFunctionType
 
 TK = 256
 H = 128
-W = 8
+W = 6
 EPS = 0.01
 DOWN = 2.0 ** -4
 N_ENGINES = 8
@@ -18,11 +18,11 @@ SCRATCH = {
     "cst": ("sbuf", [128, 4], "float32"),
     "epsv": ("sbuf", [128, W], "float32"),
     "ident": ("sbuf", [128, 128], "float32"),
-    "identn": ("sbuf", [128, 128], "float32"),
+    "idr": ("sbuf", [128, TK], "float32"),
     "mine": ("sbuf", [128, W], "float32"),
     "land1": ("sbuf", [128, 3 * W], "float32"),
     "land2": ("sbuf", [128, W], "float32"),
-    "sm": ("sbuf", [128, 96], "float32"),
+    "sm": ("sbuf", [128, 72], "float32"),
     "xT": ("sbuf", [128, TK], "float32"),
     "u": ("sbuf", [128, TK], "float32"),
     "z": ("sbuf", [128, TK], "float32"),
@@ -114,35 +114,36 @@ def rank_program(g, core, T, topo):
     def ts(o, i, s1, s2, o1, o2):
         return V.tensor_scalar(o, i, s1, s2, o1, o2)
 
+    def tt(o, a, b, op):
+        return V.tensor_tensor(o, a, b, op)
+
     LDX, LDV = [sem.ldx, 16], [sem.ldv, 16]
     ARR1, ARR2 = [sem.arr1, 3 * ne], [sem.arr2, ne]
+    WO_, RO_, SC_, RS_, WC_, RC_, BS_, W_, R_, TQ_, W2_, R2_, MAE_, XA_ = 0, 2, 4, 6, 14, 16, 54, 56, 58, 60, 62, 64, 66, 68
+    minee, KV, a6, b6, R, S, P = sm[:, 8:14], sm[:, 18:24], sm[:, 24:30], sm[:, 30:36], sm[:, 36:42], sm[:, 42:48], sm[:, 48:54]
 
     SY.dma_start(T.xs[:], T.x[:]).then_inc(sem.ldx, 16)
     ACT.dma_start(T.vs[:], T.v[:]).then_inc(sem.ldv, 16)
 
     K = stage()
-    for ap, val in ((T.cst[:, 0:1], 1.0 / D), (T.cst[:, 1:2], 0.25 / D), (T.cst[:, 2:3], -1.0 / D),
-                    (T.ident[:], 1.0), (T.identn[:], -0.5),
-                    (T.epsv[:, 0:1], EPS), (T.epsv[:, 1:2], 0.0), (T.epsv[:, 2:3], EPS), (T.epsv[:, 3:6], 0.0),
-                    (T.epsv[:, 6:8], EPS)):
+    for ap, val in ((T.cst[:, 0:1], 1.0 / D), (T.cst[:, 1:2], 2.0 / D), (T.ident[:], 1.0),
+                    (T.epsv[:, 0:4], 0.0), (T.epsv[:, 4:6], EPS)):
         do(V, [], K, lambda ap=ap, val=val: V.memset(ap, val))
-    G = stage()
-    do(g, [K], G, lambda: g.affine_select(T.identn[:], T.identn[:], [[-1, 128]], OP.is_equal, 0.0, 0, 1))
-    do(g, [], G, lambda: g.affine_select(T.ident[:], T.ident[:], [[-1, 128]], OP.is_equal, 0.0, 0, 1))
+    G = one(g, [K], lambda: g.affine_select(T.ident[:], T.ident[:], [[-1, 128]], OP.is_equal, 0.0, 0, 1))
 
     XX = [one(ACT, [LDX], lambda h=h: ACT.activation(half(T.xx, h), half(T.xs, h), FN.Square)) for h in (0, 1)]
     VV = [one(ACT, [LDV], lambda h=h: ACT.activation(half(T.vv, h), half(T.vs, h), FN.Square)) for h in (0, 1)]
-    XV = one(V, [LDX, LDV], lambda: V.tensor_tensor(T.xv[:], T.xs[:], T.vs[:], OP.mult))
+    XV = one(V, [LDX, LDV], lambda: tt(T.xv[:], T.xs[:], T.vs[:], OP.mult))
 
     PA, PBC = stage(), stage()
     for h in (0, 1):
-        do(PE, [K, XX[h]], PA, lambda h=h: PE.matmul(T.ps_a[:, 2 * h:2 * h + 2], half(T.xx, h), T.cst[:, 0:2], True, True))
+        do(PE, [K, XX[h]], PA, lambda h=h: PE.matmul(T.ps_a[:, h:h + 1], half(T.xx, h), T.cst[:, 0:1], True, True))
     for h in (0, 1):
         do(PE, [VV[h]], PBC, lambda h=h: PE.matmul(T.ps_bc[:, 2 + h:3 + h], half(T.vv, h), T.cst[:, 0:1], True, True))
     for h in (0, 1):
-        do(PE, [XV], PBC, lambda h=h: PE.matmul(T.ps_bc[:, h:h + 1], half(T.xv, h), T.cst[:, 2:3], True, True))
-    MA = one(ACT, [PA], lambda: ACT.activation(T.mine[:, 0:4], T.ps_a[:, 0:4], FN.Copy))
-    MBC = one(V, [PBC], lambda: V.tensor_copy(T.mine[:, 4:8], T.ps_bc[:, 0:4]))
+        do(PE, [XV], PBC, lambda h=h: PE.matmul(T.ps_bc[:, h:h + 1], half(T.xv, h), T.cst[:, 1:2], True, True))
+    MA = one(ACT, [PA], lambda: ACT.activation(T.mine[:, 0:2], T.ps_a[:, 0:2], FN.Copy))
+    MBC = one(V, [PBC], lambda: V.tensor_copy(T.mine[:, 2:6], T.ps_bc[:, 0:4]))
 
     g.wait_ge(MA[0], MA[1])
     g.wait_ge(MBC[0], MBC[1])
@@ -151,19 +152,23 @@ def rank_program(g, core, T, topo):
         dsts=[T.land1[:, W * near(d).index(core):W * near(d).index(core) + W] for d in peers], alu_op=0)],
         local_sem=sem.sent)
 
-    wo, ro = sm[:, 0:4], sm[:, 4:8]
-    WO = one(ACT, [MA], lambda: ACT.activation(wo, T.mine[:, 0:4], FN.Sqrt, bias=EPS, scale=1.0))
-    ME = one(V, [MA, MBC, K], lambda: V.tensor_tensor(sm[:, 8:16], T.mine[:], T.epsv[:], OP.add))
-    RO = one(V, [WO], lambda: V.reciprocal(ro, wo))
-    SC = stage()
-    for h in (0, 1):
-        do(V, [RO], SC, lambda h=h: ts(col(16, h), sm[:, 4 + 2 * h:5 + 2 * h], sm[:, 4 + 2 * h:5 + 2 * h], DOWN * DOWN,
-                                       OP.mult, OP.mult))
-        do(V, [], SC, lambda h=h: V.tensor_scalar(col(18, h), sm[:, 4 + 2 * h:5 + 2 * h], DOWN, None, OP.mult))
-
-    PX = two(PE, [G], lambda h: PE.matmul(half(T.ps_xT, h), half(T.xs, h), T.identn[:], True, True))
+    PX = two(PE, [G], lambda h: PE.matmul(half(T.ps_xT, h), half(T.xs, h), T.ident[:], True, True))
     PV = two(PE, [], lambda h: PE.matmul(half(T.ps_vT, h), half(T.vs, h), T.ident[:], True, True))
-    XT = one(ACT, [PX], lambda: ACT.activation(T.xT[:], T.ps_xT[:, 0:TK], FN.Copy))
+
+    WO = one(ACT, [MA], lambda: ACT.activation(col(WO_), T.mine[:, 0:2], FN.Sqrt, bias=EPS, scale=1.0))
+    WC = one(ACT, [MBC], lambda: ACT.activation(col(WC_), T.mine[:, 4:6], FN.Sqrt, bias=1.0 + EPS, scale=1.0))
+    ME = one(V, [MA, MBC, K], lambda: tt(minee, T.mine[:], T.epsv[:], OP.add))
+    do(V, [], ME, lambda: V.tensor_scalar(col(MAE_), T.mine[:, 0:2], EPS, None, OP.add))
+    RO = one(V, [WO], lambda: V.reciprocal(col(RO_), col(WO_)))
+    SC = two(V, [RO], lambda h: ts(col(SC_, h), col(RO_, h), col(RO_, h), DOWN * DOWN, OP.mult, OP.mult))
+    do(V, [], SC, lambda: V.tensor_scalar(col(RS_), col(RO_), DOWN, None, OP.mult))
+    RCO = one(V, [WC], lambda: V.reciprocal(col(RC_), col(WC_)))
+    K3 = one(V, [RCO], lambda: tt(sm[:, 22:24], col(RC_), col(RC_), OP.mult))
+    KK = one(V, [K3, SC], lambda: tt(sm[:, 18:20], col(SC_), sm[:, 22:24], OP.mult))
+    do(V, [], KK, lambda: tt(sm[:, 20:22], col(RS_), sm[:, 22:24], OP.mult))
+    IR0 = one(V, [G], lambda: V.tensor_scalar(half(T.idr, 0), T.ident[:], col(RC_, 0), None, OP.mult))
+    XT = two(ACT, [PX, SC], lambda h: ACT.activation(half(T.xT, h), half(T.ps_xT, h), FN.Identity, scale=col(RS_, h)))
+    IR1 = one(ACT, [G, RCO], lambda: ACT.activation(half(T.idr, 1), T.ident[:], FN.Identity, scale=col(RC_, 1)))
 
     g.wait_ge(ARR1[0], ARR1[1])
     g.remote_dma_fused([RemoteDMATransfer(
@@ -171,40 +176,29 @@ def rank_program(g, core, T, topo):
         srcs=[T.mine[:]] + [T.land1[:, W * k:W * k + W] for k in range(3)], dsts=[T.land2[:]], alu_op=1)],
         local_sem=sem.sent)
 
-    a8, b8, R, S = sm[:, 24:32], sm[:, 32:40], sm[:, 40:48], sm[:, 48:56]
     AB = stage()
-    do(V, [ARR1], AB, lambda: V.tensor_tensor(a8, T.land1[:, 0:W], T.land1[:, W:2 * W], OP.add))
-    do(V, [ME], AB, lambda: V.tensor_tensor(b8, T.land1[:, 2 * W:3 * W], sm[:, 8:16], OP.add))
-    BS = two(V, [AB, SC], lambda h: ts(col(20, h), sm[:, 24 + 2 * h:25 + 2 * h], sm[:, 32 + 2 * h:33 + 2 * h], col(16, h),
-                                       OP.add, OP.mult))
-    RR = one(V, [], lambda: V.tensor_tensor(R, a8, b8, OP.add))
+    do(V, [ARR1], AB, lambda: tt(a6, T.land1[:, 0:W], T.land1[:, W:2 * W], OP.add))
+    do(V, [ME], AB, lambda: tt(col(XA_), T.land1[:, 2 * W:2 * W + 2], col(MAE_), OP.add))
+    do(V, [], AB, lambda: tt(b6, T.land1[:, 2 * W:3 * W], minee, OP.add))
+    BS = two(V, [AB], lambda h: ts(col(BS_, h), sm[:, 24 + h:25 + h], col(XA_, h), col(SC_, h), OP.add, OP.mult))
+    RR = one(V, [], lambda: tt(R, a6, b6, OP.add))
 
-    def landed_a(h):
-        return T.land2[:, 2 * h:2 * h + 1]
-
-    WW = two(ACT, [BS, ARR2], lambda h: ACT.activation(col(56, h), landed_a(h), FN.Sqrt, bias=col(20, h), scale=col(16, h)))
-    MH = two(V, [ARR2, BS], lambda h: ts(col(58, h), landed_a(h), col(16, h), col(20, h), OP.mult, OP.add))
-    SS = one(V, [RR], lambda: V.tensor_tensor(S, R, T.land2[:], OP.add))
-    RC = one(V, [WW], lambda: V.reciprocal(col(60), col(56)))
-    EE = two(V, [RC, MH], lambda h: ts(col(62, h), col(60, h), col(58, h), col(60, h), OP.mult, OP.mult))
-    do(V, [], EE, lambda: V.tensor_tensor(col(64), col(60), col(18), OP.mult))
-    SP = two(V, [EE], lambda h: ts(col(66, h), col(62, h), 3.0, col(64, h), OP.subtract, OP.mult))
-
-    TQ = two(ACT, [SP, SS], lambda h: ACT.activation(col(68, h), sm[:, 49 + 2 * h:50 + 2 * h], FN.Identity,
-                                                     bias=sm[:, 52 + h:53 + h], scale=col(66, h)))
-    W2 = two(ACT, [TQ], lambda h: ACT.activation(col(70, h), col(68, h), FN.Sqrt, bias=sm[:, 54 + h:55 + h],
-                                                 scale=col(66, h)))
-    U0 = one(V, [SP, XT], lambda: V.tensor_scalar(half(T.u, 0), half(T.xT, 0), col(66, 0), None, OP.mult))
-    U1 = one(ACT, [XT], lambda: ACT.activation(half(T.u, 1), half(T.xT, 1), FN.Identity, scale=col(66, 1)))
-    Z0 = one(V, [U0, PV], lambda: V.tensor_tensor(half(T.z, 0), half(T.u, 0), half(T.ps_vT, 0), OP.add))
-    M2 = two(V, [TQ, SS], lambda h: ts(col(72, h), col(68, h), col(66, h), sm[:, 54 + h:55 + h], OP.mult, OP.add))
-    R2 = one(V, [W2], lambda: V.reciprocal(col(74), col(70)))
-    E2 = two(V, [R2, M2], lambda h: ts(col(76, h), col(74, h), col(72, h), col(74, h), OP.mult, OP.mult))
-    S2 = [one(V, [E2], lambda h=h: ts(col(78, h), col(76, h), 3.0, col(74, h), OP.subtract, OP.mult)) for h in (0, 1)]
-
-    DG0 = one(V, [S2[0], G], lambda: V.tensor_scalar(half(T.dg, 0), T.identn[:], col(78, 0), None, OP.mult))
-    DG1 = one(ACT, [S2[1], G], lambda: ACT.activation(half(T.dg, 1), T.identn[:], FN.Identity, scale=col(78, 1)))
-    Z1 = one(V, [U1], lambda: V.tensor_tensor(half(T.z, 1), half(T.u, 1), half(T.ps_vT, 1), OP.add))
+    WW = two(ACT, [BS, ARR2], lambda h: ACT.activation(col(W_, h), T.land2[:, h:h + 1], FN.Sqrt, bias=col(BS_, h),
+                                                       scale=col(SC_, h)))
+    SS = one(V, [ARR2, RR], lambda: tt(S, R, T.land2[:], OP.add))
+    PP = one(V, [SS, KK], lambda: tt(P, S, KV, OP.mult))
+    RC = one(V, [WW], lambda: V.reciprocal(col(R_), col(W_)))
+    TQ = two(ACT, [RC, PP], lambda h: ACT.activation(col(TQ_, h), sm[:, 48 + h:49 + h], FN.Identity,
+                                                     bias=sm[:, 50 + h:51 + h], scale=col(R_, h)))
+    W2 = two(ACT, [TQ], lambda h: ACT.activation(col(W2_, h), col(TQ_, h), FN.Sqrt, bias=sm[:, 52 + h:53 + h],
+                                                 scale=col(R_, h)))
+    U0 = one(V, [RC, XT], lambda: V.tensor_scalar(half(T.u, 0), half(T.xT, 0), col(R_, 0), None, OP.mult))
+    U1 = one(ACT, [XT], lambda: ACT.activation(half(T.u, 1), half(T.xT, 1), FN.Identity, scale=col(R_, 1)))
+    Z0 = one(V, [U0, PV], lambda: tt(half(T.z, 0), half(T.u, 0), half(T.ps_vT, 0), OP.add))
+    R2 = one(V, [W2], lambda: V.reciprocal(col(R2_), col(W2_)))
+    DG0 = one(V, [R2, IR0], lambda: V.tensor_scalar(half(T.dg, 0), half(T.idr, 0), col(R2_, 0), None, OP.mult))
+    DG1 = one(ACT, [R2, IR1], lambda: ACT.activation(half(T.dg, 1), half(T.idr, 1), FN.Identity, scale=col(R2_, 1)))
+    Z1 = one(V, [U1], lambda: tt(half(T.z, 1), half(T.u, 1), half(T.ps_vT, 1), OP.add))
     Y0 = one(PE, [DG0, Z0], lambda: PE.matmul(T.ps_y0[:, 0:H], half(T.z, 0), half(T.dg, 0), True, True))
     Y1 = one(PE, [DG1, Z1], lambda: PE.matmul(T.ps_y1[:, 0:H], half(T.z, 1), half(T.dg, 1), True, True))
     C0 = one(V, [Y0], lambda: V.tensor_copy(half(T.yo, 0), T.ps_y0[:, 0:H]))

@@ -3,11 +3,11 @@ from concourse.mybir import AluOpType, ActivationFunctionType
 
 TK = 256
 H = 128
-W = 6
+W = 8
 EPS = 0.01
 DOWN = 2.0 ** -4
 N_ENGINES = 8
-N_STAGES = 48
+N_STAGES = 64
 
 SCRATCH = {
     "xs": ("sbuf", [128, TK], "float32"),
@@ -18,12 +18,11 @@ SCRATCH = {
     "cst": ("sbuf", [128, 4], "float32"),
     "epsv": ("sbuf", [128, W], "float32"),
     "ident": ("sbuf", [128, 128], "float32"),
-    "idr": ("sbuf", [128, TK], "float32"),
     "mine": ("sbuf", [128, W], "float32"),
     "land1": ("sbuf", [128, 3 * W], "float32"),
     "land2": ("sbuf", [128, W], "float32"),
-    "sm": ("sbuf", [128, 72], "float32"),
-    "xT": ("sbuf", [128, TK], "float32"),
+    "sm": ("sbuf", [128, 96], "float32"),
+    "vT": ("sbuf", [128, TK], "float32"),
     "u": ("sbuf", [128, TK], "float32"),
     "z": ("sbuf", [128, TK], "float32"),
     "dg": ("sbuf", [128, TK], "float32"),
@@ -108,8 +107,11 @@ def rank_program(g, core, T, topo):
 
     sm = T.sm
 
-    def col(base, h=None):
-        return sm[:, base:base + 2] if h is None else sm[:, base + h:base + h + 1]
+    def cols(base, n):
+        return sm[:, base:base + n]
+
+    def col(base, k=0):
+        return sm[:, base + k:base + k + 1]
 
     def ts(o, i, s1, s2, o1, o2):
         return V.tensor_scalar(o, i, s1, s2, o1, o2)
@@ -119,15 +121,15 @@ def rank_program(g, core, T, topo):
 
     LDX, LDV = [sem.ldx, 16], [sem.ldv, 16]
     ARR1, ARR2 = [sem.arr1, 3 * ne], [sem.arr2, ne]
-    WO_, RO_, SC_, RS_, WC_, RC_, BS_, W_, R_, TQ_, W2_, R2_, MAE_, XA_ = 0, 2, 4, 6, 14, 16, 54, 56, 58, 60, 62, 64, 66, 68
-    minee, KV, a6, b6, R, S, P = sm[:, 8:14], sm[:, 18:24], sm[:, 24:30], sm[:, 30:36], sm[:, 36:42], sm[:, 42:48], sm[:, 48:54]
+    WO_, RO_, SC_, RS_, WC_, RC_, RC2_, KVA_, KVB_, RSC_ = 0, 4, 8, 10, 12, 14, 16, 18, 20, 22
+    ME_, A6_, B6_, R_, MAE_, XA_, BS_, RKA_, W_, P_, Q_, RQ_ = 24, 32, 40, 48, 56, 60, 64, 66, 68, 72, 80, 84
 
     SY.dma_start(T.xs[:], T.x[:]).then_inc(sem.ldx, 16)
     ACT.dma_start(T.vs[:], T.v[:]).then_inc(sem.ldv, 16)
 
     K = stage()
-    for ap, val in ((T.cst[:, 0:1], 1.0 / D), (T.cst[:, 1:2], 2.0 / D), (T.ident[:], 1.0),
-                    (T.epsv[:, 0:4], 0.0), (T.epsv[:, 4:6], EPS)):
+    for ap, val in ((T.cst[:, 0:2], 1.0 / D), (T.cst[:, 2:3], 2.0 / D), (T.ident[:], 1.0),
+                    (T.epsv[:, 0:6], 0.0), (T.epsv[:, 6:8], EPS)):
         do(V, [], K, lambda ap=ap, val=val: V.memset(ap, val))
     G = one(g, [K], lambda: g.affine_select(T.ident[:], T.ident[:], [[-1, 128]], OP.is_equal, 0.0, 0, 1))
 
@@ -137,13 +139,13 @@ def rank_program(g, core, T, topo):
 
     PA, PBC = stage(), stage()
     for h in (0, 1):
-        do(PE, [K, XX[h]], PA, lambda h=h: PE.matmul(T.ps_a[:, h:h + 1], half(T.xx, h), T.cst[:, 0:1], True, True))
+        do(PE, [K, XX[h]], PA, lambda h=h: PE.matmul(T.ps_a[:, 2 * h:2 * h + 2], half(T.xx, h), T.cst[:, 0:2], True, True))
     for h in (0, 1):
         do(PE, [VV[h]], PBC, lambda h=h: PE.matmul(T.ps_bc[:, 2 + h:3 + h], half(T.vv, h), T.cst[:, 0:1], True, True))
     for h in (0, 1):
-        do(PE, [XV], PBC, lambda h=h: PE.matmul(T.ps_bc[:, h:h + 1], half(T.xv, h), T.cst[:, 1:2], True, True))
-    MA = one(ACT, [PA], lambda: ACT.activation(T.mine[:, 0:2], T.ps_a[:, 0:2], FN.Copy))
-    MBC = one(V, [PBC], lambda: V.tensor_copy(T.mine[:, 2:6], T.ps_bc[:, 0:4]))
+        do(PE, [XV], PBC, lambda h=h: PE.matmul(T.ps_bc[:, h:h + 1], half(T.xv, h), T.cst[:, 2:3], True, True))
+    MA = one(ACT, [PA], lambda: ACT.activation(T.mine[:, 0:4], T.ps_a[:, 0:4], FN.Copy))
+    MBC = one(V, [PBC], lambda: V.tensor_copy(T.mine[:, 4:8], T.ps_bc[:, 0:4]))
 
     g.wait_ge(MA[0], MA[1])
     g.wait_ge(MBC[0], MBC[1])
@@ -155,20 +157,21 @@ def rank_program(g, core, T, topo):
     PX = two(PE, [G], lambda h: PE.matmul(half(T.ps_xT, h), half(T.xs, h), T.ident[:], True, True))
     PV = two(PE, [], lambda h: PE.matmul(half(T.ps_vT, h), half(T.vs, h), T.ident[:], True, True))
 
-    WO = one(ACT, [MA], lambda: ACT.activation(col(WO_), T.mine[:, 0:2], FN.Sqrt, bias=EPS, scale=1.0))
-    WC = one(ACT, [MBC], lambda: ACT.activation(col(WC_), T.mine[:, 4:6], FN.Sqrt, bias=1.0 + EPS, scale=1.0))
-    ME = one(V, [MA, MBC, K], lambda: tt(minee, T.mine[:], T.epsv[:], OP.add))
-    do(V, [], ME, lambda: V.tensor_scalar(col(MAE_), T.mine[:, 0:2], EPS, None, OP.add))
-    RO = one(V, [WO], lambda: V.reciprocal(col(RO_), col(WO_)))
-    SC = two(V, [RO], lambda h: ts(col(SC_, h), col(RO_, h), col(RO_, h), DOWN * DOWN, OP.mult, OP.mult))
-    do(V, [], SC, lambda: V.tensor_scalar(col(RS_), col(RO_), DOWN, None, OP.mult))
-    RCO = one(V, [WC], lambda: V.reciprocal(col(RC_), col(WC_)))
-    K3 = one(V, [RCO], lambda: tt(sm[:, 22:24], col(RC_), col(RC_), OP.mult))
-    KK = one(V, [K3, SC], lambda: tt(sm[:, 18:20], col(SC_), sm[:, 22:24], OP.mult))
-    do(V, [], KK, lambda: tt(sm[:, 20:22], col(RS_), sm[:, 22:24], OP.mult))
-    IR0 = one(V, [G], lambda: V.tensor_scalar(half(T.idr, 0), T.ident[:], col(RC_, 0), None, OP.mult))
-    XT = two(ACT, [PX, SC], lambda h: ACT.activation(half(T.xT, h), half(T.ps_xT, h), FN.Identity, scale=col(RS_, h)))
-    IR1 = one(ACT, [G, RCO], lambda: ACT.activation(half(T.idr, 1), T.ident[:], FN.Identity, scale=col(RC_, 1)))
+    WO = one(ACT, [MA], lambda: ACT.activation(cols(WO_, 4), T.mine[:, 0:4], FN.Sqrt, bias=EPS, scale=1.0))
+    WC = one(ACT, [MBC], lambda: ACT.activation(cols(WC_, 2), T.mine[:, 6:8], FN.Sqrt, bias=1.0 + EPS, scale=1.0))
+    ME = one(V, [MA, MBC, K], lambda: tt(cols(ME_, W), T.mine[:], T.epsv[:], OP.add))
+    do(V, [], ME, lambda: V.tensor_scalar(cols(MAE_, 4), T.mine[:, 0:4], EPS, None, OP.add))
+    RO = one(V, [WO], lambda: V.reciprocal(cols(RO_, 4), cols(WO_, 4)))
+    SC = two(V, [RO], lambda h: ts(col(SC_, h), col(RO_, 2 * h), col(RO_, 2 * h), DOWN * DOWN, OP.mult, OP.mult))
+    for h in (0, 1):
+        do(V, [], SC, lambda: V.tensor_scalar(col(RS_, h), col(RO_, 2 * h), DOWN, None, OP.mult))
+    RCO = one(V, [WC], lambda: V.reciprocal(cols(RC_, 2), cols(WC_, 2)))
+    K3 = one(V, [RCO, SC], lambda: tt(cols(RC2_, 2), cols(RC_, 2), cols(RC_, 2), OP.mult))
+    do(V, [], K3, lambda: tt(cols(RSC_, 2), cols(RS_, 2), cols(RC_, 2), OP.mult))
+    KK = one(V, [K3], lambda: tt(cols(KVA_, 2), cols(SC_, 2), cols(RC2_, 2), OP.mult))
+    do(V, [], KK, lambda: tt(cols(KVB_, 2), cols(RS_, 2), cols(RC2_, 2), OP.mult))
+    XS = two(ACT, [PX, K3], lambda h: ACT.activation(half(T.ps_xT, h), half(T.ps_xT, h), FN.Identity, scale=col(RSC_, h)))
+    VT = two(ACT, [PV, RCO, SC, KK, G], lambda h: ACT.activation(half(T.vT, h), half(T.ps_vT, h), FN.Identity, scale=col(RC_, h)))
 
     g.wait_ge(ARR1[0], ARR1[1])
     g.remote_dma_fused([RemoteDMATransfer(
@@ -177,30 +180,53 @@ def rank_program(g, core, T, topo):
         local_sem=sem.sent)
 
     AB = stage()
-    do(V, [ARR1], AB, lambda: tt(a6, T.land1[:, 0:W], T.land1[:, W:2 * W], OP.add))
-    do(V, [ME], AB, lambda: tt(col(XA_), T.land1[:, 2 * W:2 * W + 2], col(MAE_), OP.add))
-    do(V, [], AB, lambda: tt(b6, T.land1[:, 2 * W:3 * W], minee, OP.add))
-    BS = two(V, [AB], lambda h: ts(col(BS_, h), sm[:, 24 + h:25 + h], col(XA_, h), col(SC_, h), OP.add, OP.mult))
-    RR = one(V, [], lambda: tt(R, a6, b6, OP.add))
+    do(V, [ARR1, ME, KK], AB, lambda: tt(cols(A6_, W), T.land1[:, 0:W], T.land1[:, W:2 * W], OP.add))
+    do(V, [], AB, lambda: tt(cols(XA_, 4), T.land1[:, 2 * W:2 * W + 4], cols(MAE_, 4), OP.add))
+    do(V, [], AB, lambda: tt(cols(B6_, W), T.land1[:, 2 * W:3 * W], cols(ME_, W), OP.add))
+    BS = two(V, [AB], lambda h: ts(col(BS_, h), col(A6_, 2 * h), col(XA_, 2 * h), col(SC_, h), OP.add, OP.mult))
+    for h in (0, 1):
+        do(V, [], BS, lambda: ts(col(RKA_, h), col(A6_, 2 * h), col(B6_, 2 * h), col(KVA_, h), OP.add, OP.mult))
+    RR = one(V, [], lambda: tt(cols(R_, W), cols(A6_, W), cols(B6_, W), OP.add))
 
-    WW = two(ACT, [BS, ARR2], lambda h: ACT.activation(col(W_, h), T.land2[:, h:h + 1], FN.Sqrt, bias=col(BS_, h),
-                                                       scale=col(SC_, h)))
-    SS = one(V, [ARR2, RR], lambda: tt(S, R, T.land2[:], OP.add))
-    PP = one(V, [SS, KK], lambda: tt(P, S, KV, OP.mult))
-    RC = one(V, [WW], lambda: V.reciprocal(col(R_), col(W_)))
-    TQ = two(ACT, [RC, PP], lambda h: ACT.activation(col(TQ_, h), sm[:, 48 + h:49 + h], FN.Identity,
-                                                     bias=sm[:, 50 + h:51 + h], scale=col(R_, h)))
-    W2 = two(ACT, [TQ], lambda h: ACT.activation(col(W2_, h), col(TQ_, h), FN.Sqrt, bias=sm[:, 52 + h:53 + h],
-                                                 scale=col(R_, h)))
-    U0 = one(V, [RC, XT], lambda: V.tensor_scalar(half(T.u, 0), half(T.xT, 0), col(R_, 0), None, OP.mult))
-    U1 = one(ACT, [XT], lambda: ACT.activation(half(T.u, 1), half(T.xT, 1), FN.Identity, scale=col(R_, 1)))
-    Z0 = one(V, [U0, PV], lambda: tt(half(T.z, 0), half(T.u, 0), half(T.ps_vT, 0), OP.add))
-    R2 = one(V, [W2], lambda: V.reciprocal(col(R2_), col(W2_)))
-    DG0 = one(V, [R2, IR0], lambda: V.tensor_scalar(half(T.dg, 0), half(T.idr, 0), col(R2_, 0), None, OP.mult))
-    DG1 = one(ACT, [R2, IR1], lambda: ACT.activation(half(T.dg, 1), half(T.idr, 1), FN.Identity, scale=col(R2_, 1)))
-    Z1 = one(V, [U1], lambda: tt(half(T.z, 1), half(T.u, 1), half(T.ps_vT, 1), OP.add))
-    Y0 = one(PE, [DG0, Z0], lambda: PE.matmul(T.ps_y0[:, 0:H], half(T.z, 0), half(T.dg, 0), True, True))
-    Y1 = one(PE, [DG1, Z1], lambda: PE.matmul(T.ps_y1[:, 0:H], half(T.z, 1), half(T.dg, 1), True, True))
+    WP = []
+    for h in (0, 1):
+        st = stage()
+        do(ACT, [BS, ARR2] if h == 0 else [], st,
+           lambda: ACT.activation(cols(W_ + 2 * h, 2), T.land2[:, 2 * h:2 * h + 2], FN.Sqrt, bias=col(BS_, h), scale=col(SC_, h)))
+        do(ACT, [], st,
+           lambda: ACT.activation(col(P_ + 4 * h, 2), T.land2[:, 2 * h:2 * h + 1], FN.Identity, bias=col(RKA_, h), scale=col(KVA_, h)))
+        WP.append(st)
+    PV_ = []
+    for h in (0, 1):
+        st = stage()
+        do(V, [ARR2, RR] if h == 0 else [], st,
+           lambda: ts(col(P_ + 4 * h, 0), T.land2[:, 6 + h:7 + h], col(R_, 6 + h), col(RC2_, h), OP.add, OP.mult))
+        do(V, [], st,
+           lambda: ts(col(P_ + 4 * h, 1), T.land2[:, 4 + h:5 + h], col(R_, 4 + h), col(KVB_, h), OP.add, OP.mult))
+        PV_.append(st)
+
+    def scan(h):
+        return one(V, [PV_[h], WP[h]], lambda: V.tensor_tensor_scan(cols(Q_ + 2 * h, 2), cols(W_ + 2 * h, 2), cols(P_ + 4 * h + 1, 2),
+                                                                    col(P_ + 4 * h, 0), OP.mult, OP.add))
+
+    def recip(h, dep):
+        return one(V, [dep], lambda: V.reciprocal(col(RQ_, h), col(Q_ + 2 * h, 1)))
+
+    def zsum(h):
+        return one(V, [U[h]] + ([XS] if h == 0 else []), lambda: tt(half(T.z, h), half(T.u, h), half(T.ps_xT, h), OP.add))
+
+    U = [one(ACT, [WP[h], VT], lambda: ACT.activation(half(T.u, h), half(T.vT, h), FN.Identity, scale=col(W_ + 2 * h, 0)))
+         for h in (0, 1)]
+    Q0 = scan(0)
+    R0 = recip(0, Q0)
+    Q1 = scan(1)
+    Z0 = zsum(0)
+    R1 = recip(1, Q1)
+    Z1 = zsum(1)
+    DG = [one(ACT, [r_], lambda: ACT.activation(half(T.dg, h), T.ident[:], FN.Sqrt, scale=col(RQ_, h)))
+          for h, r_ in ((0, R0), (1, R1))]
+    Y0 = one(PE, [DG[0], Z0], lambda: PE.matmul(T.ps_y0[:, 0:H], half(T.z, 0), half(T.dg, 0), True, True))
+    Y1 = one(PE, [DG[1], Z1], lambda: PE.matmul(T.ps_y1[:, 0:H], half(T.z, 1), half(T.dg, 1), True, True))
     C0 = one(V, [Y0], lambda: V.tensor_copy(half(T.yo, 0), T.ps_y0[:, 0:H]))
     SY.wait_ge(C0[0], C0[1])
     SY.dma_start(half(T.y, 0), half(T.yo, 0)).then_inc(sem.st0, 16)

from concourse.bass import DstId, RemoteDMATransfer
from concourse.mybir import AluOpType, ActivationFunctionType

TK = 256
H = 128
W = 8
EPS = 0.01
DOWN = 2.0 ** -4
N_ENGINES = 8
N_STAGES = 64

SCRATCH = {
    "xs": ("sbuf", [128, TK], "float32"),
    "vs": ("sbuf", [128, TK], "float32"),
    "xx": ("sbuf", [128, TK], "float32"),
    "xv": ("sbuf", [128, TK], "float32"),
    "vv": ("sbuf", [128, TK], "float32"),
    "cst": ("sbuf", [128, 4], "float32"),
    "epsv": ("sbuf", [128, W], "float32"),
    "ident": ("sbuf", [128, 128], "float32"),
    "mine": ("sbuf", [128, W], "float32"),
    "land1": ("sbuf", [128, 3 * W], "float32"),
    "land2": ("sbuf", [128, W], "float32"),
    "sm": ("sbuf", [128, 96], "float32"),
    "vT": ("sbuf", [128, TK], "float32"),
    "u": ("sbuf", [128, TK], "float32"),
    "z": ("sbuf", [128, TK], "float32"),
    "dg": ("sbuf", [128, TK], "float32"),
    "yo": ("sbuf", [128, TK], "float32"),
    "ps_a": ("psum", [128, 512], "float32"),
    "ps_bc": ("psum", [128, 512], "float32"),
    "ps_xT": ("psum", [128, 512], "float32"),
    "ps_vT": ("psum", [128, 512], "float32"),
    "ps_y0": ("psum", [128, 512], "float32"),
    "ps_y1": ("psum", [128, 512], "float32"),
}
SEMAPHORES = ["ldx", "ldv", "arr1", "arr2", "sent", "st0", "st1"] + ["s%d" % i for i in range(N_STAGES)]


def _some_engines(mask, n):
    out, b = 0, 1
    while n and b <= mask:
        if mask & b:
            out |= b
            n -= 1
        b <<= 1
    return out


def rank_program(g, core, T, topo):
    if T.rank_of(core) is None:
        return
    OP, FN = AluOpType, ActivationFunctionType
    sem = T.sem
    V, ACT, PE, SY = g.vector, g.scalar, g.tensor, g.sync
    grp = list(T.cores)
    D = 128 * len(grp)

    def rack(c):
        return topo.rack(topo.host(c))

    def near(c):
        return [d for d in grp if d != c and rack(d) == rack(c)]

    def hops(d):
        return 2 if topo.mates(core, d) else (1 if topo.same_plane(core, d) else 0)

    peers = sorted(near(core), key=hops)
    far = [d for d in grp if rack(d) != rack(core) and topo.chip(d) == topo.chip(core) and topo.may_write(core, d)][0]

    def dst(d):
        rid, pid = topo.addr(d, core)
        return DstId(rid=rid, pnc=pid)

    m1 = topo.mask(core, far)
    for d in peers:
        m1 &= topo.mask(core, d)
    mask = _some_engines(m1, N_ENGINES)
    ne = bin(mask).count("1")

    stages = []

    def stage():
        st = [sem["s%d" % len(stages)], 0]
        stages.append(st)
        return st

    def do(q, deps, st, fn):
        for d in deps:
            q.wait_ge(d[0], d[1])
        fn().then_inc(st[0], 1)
        st[1] += 1

    def one(q, deps, fn):
        st = stage()
        do(q, deps, st, fn)
        return st

    def two(q, deps, fn):
        st = stage()
        do(q, deps, st, lambda: fn(0))
        do(q, [], st, lambda: fn(1))
        return st

    def half(t_, h):
        return t_[:, h * H:(h + 1) * H]

    sm = T.sm

    def cols(base, n):
        return sm[:, base:base + n]

    def col(base, k=0):
        return sm[:, base + k:base + k + 1]

    def ts(o, i, s1, s2, o1, o2):
        return V.tensor_scalar(o, i, s1, s2, o1, o2)

    def tt(o, a, b, op):
        return V.tensor_tensor(o, a, b, op)

    LDX, LDV = [sem.ldx, 16], [sem.ldv, 16]
    ARR1, ARR2 = [sem.arr1, 3 * ne], [sem.arr2, ne]
    WO_, RO_, SC_, RS_, WC_, RC_, RC2_, KVA_, KVB_, RSC_ = 0, 4, 8, 10, 12, 14, 16, 18, 20, 22
    ME_, A6_, B6_, R_, MAE_, XA_, BS_, RKA_, W_, P_, Q_, RQ_ = 24, 32, 40, 48, 56, 60, 64, 66, 68, 72, 80, 84

    SY.dma_start(T.xs[:], T.x[:]).then_inc(sem.ldx, 16)
    ACT.dma_start(T.vs[:], T.v[:]).then_inc(sem.ldv, 16)

    K = stage()
    for ap, val in ((T.cst[:, 0:2], 1.0 / D), (T.cst[:, 2:3], 2.0 / D), (T.ident[:], 1.0),
                    (T.epsv[:, 0:6], 0.0), (T.epsv[:, 6:8], EPS)):
        do(V, [], K, lambda ap=ap, val=val: V.memset(ap, val))
    G = one(g, [K], lambda: g.affine_select(T.ident[:], T.ident[:], [[-1, 128]], OP.is_equal, 0.0, 0, 1))

    XX = [one(ACT, [LDX], lambda h=h: ACT.activation(half(T.xx, h), half(T.xs, h), FN.Square)) for h in (0, 1)]
    VV = [one(ACT, [LDV], lambda h=h: ACT.activation(half(T.vv, h), half(T.vs, h), FN.Square)) for h in (0, 1)]
    XV = one(V, [LDX, LDV], lambda: tt(T.xv[:], T.xs[:], T.vs[:], OP.mult))

    PA, PBC = stage(), stage()
    for h in (0, 1):
        do(PE, [K, XX[h]], PA, lambda h=h: PE.matmul(T.ps_a[:, 2 * h:2 * h + 2], half(T.xx, h), T.cst[:, 0:2], True, True))
    for h in (0, 1):
        do(PE, [VV[h]], PBC, lambda h=h: PE.matmul(T.ps_bc[:, 2 + h:3 + h], half(T.vv, h), T.cst[:, 0:1], True, True))
    for h in (0, 1):
        do(PE, [XV], PBC, lambda h=h: PE.matmul(T.ps_bc[:, h:h + 1], half(T.xv, h), T.cst[:, 2:3], True, True))
    MA = one(ACT, [PA], lambda: ACT.activation(T.mine[:, 0:4], T.ps_a[:, 0:4], FN.Copy))
    MBC = one(V, [PBC], lambda: V.tensor_copy(T.mine[:, 4:8], T.ps_bc[:, 0:4]))

    g.wait_ge(MA[0], MA[1])
    g.wait_ge(MBC[0], MBC[1])
    g.remote_dma_fused([RemoteDMATransfer(
        dst_ids=[dst(d) for d in peers], dma_engine_mask=mask, remote_sem=sem.arr1, srcs=[T.mine[:]],
        dsts=[T.land1[:, W * near(d).index(core):W * near(d).index(core) + W] for d in peers], alu_op=0)],
        local_sem=sem.sent)

    PX = two(PE, [G], lambda h: PE.matmul(half(T.ps_xT, h), half(T.xs, h), T.ident[:], True, True))
    PV = two(PE, [], lambda h: PE.matmul(half(T.ps_vT, h), half(T.vs, h), T.ident[:], True, True))

    WO = one(ACT, [MA], lambda: ACT.activation(cols(WO_, 4), T.mine[:, 0:4], FN.Sqrt, bias=EPS, scale=1.0))
    WC = one(ACT, [MBC], lambda: ACT.activation(cols(WC_, 2), T.mine[:, 6:8], FN.Sqrt, bias=1.0 + EPS, scale=1.0))
    ME = one(V, [MA, MBC, K], lambda: tt(cols(ME_, W), T.mine[:], T.epsv[:], OP.add))
    do(V, [], ME, lambda: V.tensor_scalar(cols(MAE_, 4), T.mine[:, 0:4], EPS, None, OP.add))
    RO = one(V, [WO], lambda: V.reciprocal(cols(RO_, 4), cols(WO_, 4)))
    SC = two(V, [RO], lambda h: ts(col(SC_, h), col(RO_, 2 * h), col(RO_, 2 * h), DOWN * DOWN, OP.mult, OP.mult))
    for h in (0, 1):
        do(V, [], SC, lambda: V.tensor_scalar(col(RS_, h), col(RO_, 2 * h), DOWN, None, OP.mult))
    RCO = one(V, [WC], lambda: V.reciprocal(cols(RC_, 2), cols(WC_, 2)))
    K3 = one(V, [RCO, SC], lambda: tt(cols(RC2_, 2), cols(RC_, 2), cols(RC_, 2), OP.mult))
    do(V, [], K3, lambda: tt(cols(RSC_, 2), cols(RS_, 2), cols(RC_, 2), OP.mult))
    KK = one(V, [K3], lambda: tt(cols(KVA_, 2), cols(SC_, 2), cols(RC2_, 2), OP.mult))
    do(V, [], KK, lambda: tt(cols(KVB_, 2), cols(RS_, 2), cols(RC2_, 2), OP.mult))
    XS = two(ACT, [PX, K3], lambda h: ACT.activation(half(T.ps_xT, h), half(T.ps_xT, h), FN.Identity, scale=col(RSC_, h)))
    VT = two(ACT, [PV, RCO, SC, KK, G], lambda h: ACT.activation(half(T.vT, h), half(T.ps_vT, h), FN.Identity, scale=col(RC_, h)))

    g.wait_ge(ARR1[0], ARR1[1])
    g.remote_dma_fused([RemoteDMATransfer(
        dst_ids=[dst(far)], dma_engine_mask=mask, remote_sem=sem.arr2,
        srcs=[T.mine[:]] + [T.land1[:, W * k:W * k + W] for k in range(3)], dsts=[T.land2[:]], alu_op=1)],
        local_sem=sem.sent)

    AB = stage()
    do(V, [ARR1, ME, KK], AB, lambda: tt(cols(A6_, W), T.land1[:, 0:W], T.land1[:, W:2 * W], OP.add))
    do(V, [], AB, lambda: tt(cols(XA_, 4), T.land1[:, 2 * W:2 * W + 4], cols(MAE_, 4), OP.add))
    do(V, [], AB, lambda: tt(cols(B6_, W), T.land1[:, 2 * W:3 * W], cols(ME_, W), OP.add))
    BS = two(V, [AB], lambda h: ts(col(BS_, h), col(A6_, 2 * h), col(XA_, 2 * h), col(SC_, h), OP.add, OP.mult))
    for h in (0, 1):
        do(V, [], BS, lambda: ts(col(RKA_, h), col(A6_, 2 * h), col(B6_, 2 * h), col(KVA_, h), OP.add, OP.mult))
    RR = one(V, [], lambda: tt(cols(R_, W), cols(A6_, W), cols(B6_, W), OP.add))

    WP = []
    for h in (0, 1):
        st = stage()
        do(ACT, [BS, ARR2] if h == 0 else [], st,
           lambda: ACT.activation(cols(W_ + 2 * h, 2), T.land2[:, 2 * h:2 * h + 2], FN.Sqrt, bias=col(BS_, h), scale=col(SC_, h)))
        do(ACT, [], st,
           lambda: ACT.activation(col(P_ + 4 * h, 2), T.land2[:, 2 * h:2 * h + 1], FN.Identity, bias=col(RKA_, h), scale=col(KVA_, h)))
        WP.append(st)
    PV_ = []
    for h in (0, 1):
        st = stage()
        do(V, [ARR2, RR] if h == 0 else [], st,
           lambda: ts(col(P_ + 4 * h, 0), T.land2[:, 6 + h:7 + h], col(R_, 6 + h), col(RC2_, h), OP.add, OP.mult))
        do(V, [], st,
           lambda: ts(col(P_ + 4 * h, 1), T.land2[:, 4 + h:5 + h], col(R_, 4 + h), col(KVB_, h), OP.add, OP.mult))
        PV_.append(st)

    def scan(h):
        return one(V, [PV_[h], WP[h]], lambda: V.tensor_tensor_scan(cols(Q_ + 2 * h, 2), cols(W_ + 2 * h, 2), cols(P_ + 4 * h + 1, 2),
                                                                    col(P_ + 4 * h, 0), OP.mult, OP.add))

    def recip(h, dep):
        return one(V, [dep], lambda: V.reciprocal(col(RQ_, h), col(Q_ + 2 * h, 1)))

    def zsum(h):
        return one(V, [U[h]] + ([XS] if h == 0 else []), lambda: tt(half(T.z, h), half(T.u, h), half(T.ps_xT, h), OP.add))

    U = [one(ACT, [WP[h], VT], lambda: ACT.activation(half(T.u, h), half(T.vT, h), FN.Identity, scale=col(W_ + 2 * h, 0)))
         for h in (0, 1)]
    Q0 = scan(0)
    R0 = recip(0, Q0)
    Q1 = scan(1)
    Z0 = zsum(0)
    R1 = recip(1, Q1)
    Z1 = zsum(1)
    DG = [one(ACT, [r_], lambda: ACT.activation(half(T.dg, h), T.ident[:], FN.Sqrt, scale=col(RQ_, h)))
          for h, r_ in ((0, R0), (1, R1))]
    Y0 = one(PE, [DG[0], Z0], lambda: PE.matmul(T.ps_y0[:, 0:H], half(T.z, 0), half(T.dg, 0), True, True))
    Y1 = one(PE, [DG[1], Z1], lambda: PE.matmul(T.ps_y1[:, 0:H], half(T.z, 1), half(T.dg, 1), True, True))
    C0 = one(V, [Y0], lambda: V.tensor_copy(half(T.yo, 0), T.ps_y0[:, 0:H]))
    SY.wait_ge(C0[0], C0[1])
    SY.dma_start(half(T.y, 0), half(T.yo, 0)).then_inc(sem.st0, 16)
    C1 = one(ACT, [Y1], lambda: ACT.activation(half(T.yo, 1), T.ps_y1[:, 0:H], FN.Copy))
    ACT.wait_ge(C1[0], C1[1])
    ACT.dma_start(half(T.y, 1), half(T.yo, 1)).then_inc(sem.st1, 16)

    g.wait_ge(sem.sent, 2 * ne)
    for st in stages:
        g.wait_ge(st[0], st[1])
    g.wait_ge(sem.st0, 16)
    g.wait_ge(sem.st1, 16)
